import numpy as np
import ml_dtypes


def mxq(x, axis, fmt="e4m3"):
    dtype, down = {"e4m3": (ml_dtypes.float8_e4m3fn, 7), "e5m2": (ml_dtypes.float8_e5m2, 14)}[fmt]
    v = np.moveaxis(np.asarray(x, np.float32).astype(ml_dtypes.bfloat16).astype(np.float64), axis, -1)
    blocks = v.reshape(v.shape[:-1] + (-1, 32))
    amax = np.abs(blocks).max(-1, keepdims=True)
    byte = np.maximum(np.where(amax > 0, np.frexp(amax)[1] - 1 + 127, 0) - down, 1)
    scale = np.exp2(byte - 127.0)
    codes = (blocks / scale).astype(np.float32).astype(dtype).astype(np.float64)
    return np.moveaxis((codes * scale).reshape(v.shape), -1, axis)


WIDE = False


def mx_kscale(k, group=512):
    if not WIDE:
        return np.ones(k)
    levels = np.array([18, -18])
    if group != 512:
        return np.exp2(np.random.permutation(np.resize(levels, k // group))).repeat(group)
    if k % 512:
        return np.exp2(np.random.permutation(np.resize(levels, k // 32))).repeat(32)
    a = np.empty((k // 512, 16))
    for p in range(k // 512):
        a[p, :8] = np.random.permutation(np.resize(levels, 8))
        for g in range(8):
            far = levels[np.abs(levels - a[p, g]) >= 10]
            a[p, g + 8] = far[np.random.randint(len(far))]
    return np.exp2(a.ravel()).repeat(32)


def f64(x):
    return np.asarray(x).astype(np.float64)


E2M1 = np.array([0.0, 0.5, 1.0, 1.5, 2.0, 3.0, 4.0, 6.0, -0.0, -0.5, -1.0, -1.5, -2.0, -3.0, -4.0, -6.0])


def pack_group(w):
    k, n = w.shape
    w = f64(np.asarray(w, np.float32).astype(ml_dtypes.bfloat16)).reshape(k // 32, 32, n)
    amax = np.abs(w).max(1)
    mant, ex = np.frexp(amax / 6.0)
    byte = np.clip(np.where(amax > 0, np.where(mant > 0.5, ex, ex - 1) + 127, 1), 1, 254)
    scaled = (w * np.exp2(127.0 - byte)[:, None, :]).reshape(k, n).astype(np.float32)
    c = np.ascontiguousarray(scaled.reshape(k // 4, 4, n).transpose(0, 2, 1)).astype(ml_dtypes.float4_e2m1fn).view(np.uint8) & 0xF
    return np.ascontiguousarray((c[..., 0::2] | (c[..., 1::2] << 4)).reshape(k // 4, 2 * n)), byte.astype(np.uint8)


def unpack_group(words, scales):
    p, n = words.shape[0], scales.shape[1]
    words = np.ascontiguousarray(words).reshape(p, n, 2)
    nib = np.empty((p, n, 4), np.uint8)
    nib[..., 0::2] = words & 0xF
    nib[..., 1::2] = words >> 4
    return E2M1[nib].transpose(0, 2, 1).reshape(4 * p, n) * np.repeat(np.exp2(scales.astype(np.float64) - 127.0), 32, axis=0)


G, D, M, N = 8, 128, 128, 512


def setup_inputs():
    n = np.random.standard_normal
    s = mx_kscale(D, 0)[:, None]
    w_ = [pack_group(w) for w in n((G, D, M)) / np.sqrt(D) / s]
    return {
        "x": (n((G, D, N)) * s).astype(np.float32),
        "w_words": np.stack([w[0] for w in w_]),
        "w_scales": np.stack([w[1] for w in w_]),
        "b": (0.5 * n((G, M, 1))).astype(np.float32),
    }


def reference(x, w_words, w_scales, b):
    xq = mxq(f64(x), 1, "e4m3")
    y = np.stack([unpack_group(w_words[g], w_scales[g]) for g in range(G)]).transpose(0, 2, 1) @ xq
    y = y + f64(b)
    y = np.square(np.maximum(y, 0.0))
    return y

@@ -1,0 +1,130 @@
+from contextlib import ExitStack
+
+import concourse.mybir as mybir
+
+G, D, M, N = 8, 128, 128, 512
+FLOPS = 2 * G * D * M * N
+
+F32 = mybir.dt.float32
+BF16 = mybir.dt.bfloat16
+I32 = mybir.dt.int32
+U32 = mybir.dt.uint32
+U8 = mybir.dt.uint8
+FP8X4 = mybir.dt.float8_e4m3fn_x4
+FP4X4 = mybir.dt.float4_e2m1fn_x4
+ALU = mybir.AluOpType
+ACT = mybir.ActivationFunctionType
+
+P = 128
+PACK = 4
+ROWS = 32
+TILES = 4
+SETS = 2
+
+
+def tile_rows_glin_relu2_bias_kernel(tc, x, w_words, w_scales, b, out):
+    nc = tc.nc
+    with ExitStack() as ctx:
+        keep = ctx.enter_context(tc.tile_pool(name="keep", bufs=1))
+        psum = ctx.enter_context(tc.psum_pool(name="psum", bufs=1))
+        ctx.enter_context(tc.manual_schedule())
+
+        raw = [keep.tile([P, PACK * N], F32, name="raw%d" % s) for s in range(SETS)]
+        grouped = [keep.tile([P, PACK * N], BF16, name="grouped%d" % s, align_bytes=64) for s in range(SETS)]
+        codes = [keep.tile([P, N], U32, name="codes%d" % s, align_bytes=64) for s in range(SETS)]
+        scales = [keep.tile([P, N], U8, name="scales%d" % s, align_bytes=64) for s in range(SETS)]
+        w_sb = keep.tile([P, SETS, 2 * M], U8, align_bytes=64)
+        ws_sb = keep.tile([P, SETS, M], U8, align_bytes=64)
+        b_rows = keep.tile([P, G * ROWS], F32, align_bytes=64)
+        b_cols = keep.tile([P, G * ROWS], F32, align_bytes=64)
+        acc = [psum.tile([M, N], F32, name="acc%d" % g) for g in range(G)]
+        relu = [keep.tile([M, N], F32, name="relu%d" % g) for g in range(G)]
+        res = [keep.tile([M, N], F32, name="res%d" % g) for g in range(G)]
+
+        x_sets = x.rearrange("(s c) (p j) n -> s (c p) (j n)", c=TILES, j=PACK)
+        ws_tiles = w_scales.rearrange("(s c) f m -> c f s m", c=TILES)
+
+        nc.vector.memset(ws_sb[:].bitcast(U32), 0)
+        nc.vector.memset(b_rows[:], 0.0)
+
+        nc.sync.dma_start(out=raw[0][:], in_=x_sets[0])
+        nc.sync.dma_start(out=w_sb[:].bitcast(I32), in_=w_words.rearrange("(s c) p v -> (c p) s v", c=TILES).bitcast(I32))
+        for c in range(TILES):
+            nc.sync.dma_start(out=ws_sb[ROWS * c : ROWS * c + 4].bitcast(I32), in_=ws_tiles[c].bitcast(I32))
+        nc.sync.dma_start(out=raw[1][:], in_=x_sets[1])
+        nc.scalar.dma_start(
+            out=b_rows[0:P:ROWS, :].rearrange("q (g a) -> q g a", a=ROWS),
+            in_=b.rearrange("g (q a) o -> q g (a o)", a=ROWS),
+        )
+        nc.vector.transpose(b_cols[:], b_rows[:])
+
+        def interleave(copy, s, n0, n1):
+            dst = grouped[s][:].rearrange("p (c i t) -> p c t i", i=4, t=PACK)
+            src = raw[s][:].rearrange("p (t c i) -> p c t i", i=4, t=PACK)
+            copy(out=dst[:, n0 // 4 : n1 // 4], in_=src[:, n0 // 4 : n1 // 4])
+
+        def quantize(s, n0, n1):
+            nc.vector.quantize_mx(
+                out=codes[s][:, n0:n1].bitcast(FP8X4),
+                scales=scales[s][:, n0:n1],
+                in_=grouped[s][:, PACK * n0 : PACK * n1],
+            )
+
+        def multiply(s):
+            for c in range(TILES):
+                rows = slice(ROWS * c, ROWS * (c + 1))
+                nc.tensor.matmul_mx(
+                    out=acc[TILES * s + c][:],
+                    lhsT=w_sb[rows, s, :].bitcast(FP4X4),
+                    lhsT_scale=ws_sb[rows, s, :],
+                    rhs=codes[s][rows, :].bitcast(FP8X4),
+                    rhs_scale=scales[s][rows, :],
+                    start=True,
+                    stop=True,
+                )
+
+        def bias(g):
+            return b_cols[:, ROWS * g : ROWS * g + 1]
+
+        def relu_v(g):
+            nc.vector.tensor_scalar(out=relu[g][:], in0=acc[g][:], scalar1=bias(g), scalar2=0.0, op0=ALU.add, op1=ALU.max)
+
+        def relu_s(g):
+            nc.scalar.activation(out=relu[g][:], in_=acc[g][:], func=ACT.Relu, bias=bias(g))
+
+        def square_v(g):
+            nc.vector.tensor_tensor(out=res[g][:], in0=relu[g][:], in1=relu[g][:], op=ALU.mult)
+            nc.sync.dma_start(out=out[g], in_=res[g][:])
+
+        def square_s(g):
+            nc.scalar.activation(out=res[g][:], in_=relu[g][:], func=ACT.Square)
+            nc.sync.dma_start(out=out[g], in_=res[g][:])
+
+        interleave(nc.scalar.copy, 0, 320, 512)
+        interleave(nc.vector.tensor_copy, 0, 0, 256)
+        interleave(nc.vector.tensor_copy, 0, 256, 320)
+        quantize(0, 0, 256)
+        quantize(0, 256, 512)
+        multiply(0)
+
+        relu_v(0)
+        relu_s(1)
+        square_s(0)
+        interleave(nc.vector.tensor_copy, 1, 0, 256)
+        interleave(nc.vector.tensor_copy, 1, 256, 512)
+        quantize(1, 0, 256)
+        quantize(1, 256, 512)
+        multiply(1)
+        relu_s(2)
+        square_s(1)
+        relu_v(3)
+        square_s(2)
+        relu_v(4)
+        square_s(3)
+        relu_v(5)
+        square_s(4)
+        relu_v(6)
+        square_s(5)
+        relu_v(7)
+        square_s(6)
+        square_v(7)

@@ -20,6 +20,8 @@ PACK = 4
 ROWS = 32
 TILES = 4
 SETS = 2
+W = 256
+CHUNKS = 4
 
 
 def tile_rows_glin_relu2_bias_kernel(tc, x, w_words, w_scales, b, out):
@@ -29,102 +31,115 @@ def tile_rows_glin_relu2_bias_kernel(tc, x, w_words, w_scales, b, out):
         psum = ctx.enter_context(tc.psum_pool(name="psum", bufs=1))
         ctx.enter_context(tc.manual_schedule())
 
-        raw = [keep.tile([P, PACK * N], F32, name="raw%d" % s) for s in range(SETS)]
-        grouped = [keep.tile([P, PACK * N], BF16, name="grouped%d" % s, align_bytes=64) for s in range(SETS)]
-        codes = [keep.tile([P, N], U32, name="codes%d" % s, align_bytes=64) for s in range(SETS)]
-        scales = [keep.tile([P, N], U8, name="scales%d" % s, align_bytes=64) for s in range(SETS)]
+        raw = [keep.tile([P, PACK, W], F32, name="raw%d" % k) for k in range(CHUNKS)]
+        grouped = [keep.tile([P, PACK * W], BF16, name="grouped%d" % k, align_bytes=64) for k in range(CHUNKS)]
+        codes = keep.tile([P, (CHUNKS + 1) * W], U32, align_bytes=64)
+        scales = keep.tile([P, (CHUNKS + 1) * W], U8, align_bytes=64)
         w_sb = keep.tile([P, SETS, 2 * M], U8, align_bytes=64)
         ws_sb = keep.tile([P, SETS, M], U8, align_bytes=64)
         b_rows = keep.tile([P, G * ROWS], F32, align_bytes=64)
         b_cols = keep.tile([P, G * ROWS], F32, align_bytes=64)
-        acc = [psum.tile([M, N], F32, name="acc%d" % g) for g in range(G)]
-        relu = [keep.tile([M, N], F32, name="relu%d" % g) for g in range(G)]
-        res = [keep.tile([M, N], F32, name="res%d" % g) for g in range(G)]
+        acc = [[psum.tile([M, N], F32, name="acc%d_%d" % (h, c)) for c in range(TILES)] for h in range(2)]
+        relu = [keep.tile([M, TILES * W], F32, name="relu%d" % k) for k in range(CHUNKS)]
+        res = [keep.tile([M, TILES * W], F32, name="res%d" % k) for k in range(CHUNKS)]
 
-        x_sets = x.rearrange("(s c) (p j) n -> s (c p) (j n)", c=TILES, j=PACK)
+        x_sets = x.rearrange("(s c) (p j) n -> s (c p) j n", c=TILES, j=PACK)
         ws_tiles = w_scales.rearrange("(s c) f m -> c f s m", c=TILES)
 
         nc.vector.memset(ws_sb[:].bitcast(U32), 0)
         nc.vector.memset(b_rows[:], 0.0)
+        nc.vector.memset(codes[:, 0:W], 0)
+        nc.vector.memset(scales[:, 0:W].bitcast(U32), 0)
 
-        nc.sync.dma_start(out=raw[0][:], in_=x_sets[0])
+        def load_x(k):
+            nc.sync.dma_start(out=raw[k][:], in_=x_sets[k // 2][:, :, W * (k % 2) : W * (k % 2 + 1)])
+
+        load_x(0)
         nc.sync.dma_start(out=w_sb[:].bitcast(I32), in_=w_words.rearrange("(s c) p v -> (c p) s v", c=TILES).bitcast(I32))
         for c in range(TILES):
             nc.sync.dma_start(out=ws_sb[ROWS * c : ROWS * c + 4].bitcast(I32), in_=ws_tiles[c].bitcast(I32))
-        nc.sync.dma_start(out=raw[1][:], in_=x_sets[1])
         nc.scalar.dma_start(
             out=b_rows[0:P:ROWS, :].rearrange("q (g a) -> q g a", a=ROWS),
             in_=b.rearrange("g (q a) o -> q g (a o)", a=ROWS),
         )
-        nc.vector.transpose(b_cols[:], b_rows[:])
+        for k in range(1, CHUNKS):
+            load_x(k)
 
-        def interleave(copy, s, n0, n1):
-            dst = grouped[s][:].rearrange("p (c i t) -> p c t i", i=4, t=PACK)
-            src = raw[s][:].rearrange("p (t c i) -> p c t i", i=4, t=PACK)
+        def interleave(copy, k, n0, n1):
+            dst = grouped[k][:].rearrange("p (c i t) -> p c t i", i=4, t=PACK)
+            src = raw[k][:].rearrange("p t (c i) -> p c t i", i=4)
             copy(out=dst[:, n0 // 4 : n1 // 4], in_=src[:, n0 // 4 : n1 // 4])
 
-        def quantize(s, n0, n1):
+        def quantize_and_multiply(k):
             nc.vector.quantize_mx(
-                out=codes[s][:, n0:n1].bitcast(FP8X4),
-                scales=scales[s][:, n0:n1],
-                in_=grouped[s][:, PACK * n0 : PACK * n1],
+                out=codes[:, W * (k + 1) : W * (k + 2)].bitcast(FP8X4),
+                scales=scales[:, W * (k + 1) : W * (k + 2)],
+                in_=grouped[k][:],
             )
-
-        def multiply(s):
+            window = slice(W * k, W * k + N)
             for c in range(TILES):
                 rows = slice(ROWS * c, ROWS * (c + 1))
                 nc.tensor.matmul_mx(
-                    out=acc[TILES * s + c][:],
-                    lhsT=w_sb[rows, s, :].bitcast(FP4X4),
-                    lhsT_scale=ws_sb[rows, s, :],
-                    rhs=codes[s][rows, :].bitcast(FP8X4),
-                    rhs_scale=scales[s][rows, :],
+                    out=acc[k % 2][c][:],
+                    lhsT=w_sb[rows, k // 2, :].bitcast(FP4X4),
+                    lhsT_scale=ws_sb[rows, k // 2, :],
+                    rhs=codes[rows, window].bitcast(FP8X4),
+                    rhs_scale=scales[rows, window],
                     start=True,
                     stop=True,
                 )
 
-        def bias(g):
+        def bias(k, c):
+            g = TILES * (k // 2) + c
             return b_cols[:, ROWS * g : ROWS * g + 1]
 
-        def relu_v(g):
-            nc.vector.tensor_scalar(out=relu[g][:], in0=acc[g][:], scalar1=bias(g), scalar2=0.0, op0=ALU.add, op1=ALU.max)
+        def relu_v(k, c):
+            nc.vector.tensor_scalar(out=relu[k][:, W * c : W * (c + 1)], in0=acc[k % 2][c][:, W:N], scalar1=bias(k, c), scalar2=0.0, op0=ALU.add, op1=ALU.max)
 
-        def relu_s(g):
-            nc.scalar.activation(out=relu[g][:], in_=acc[g][:], func=ACT.Relu, bias=bias(g))
+        def relu_s(k, c):
+            nc.scalar.activation(out=relu[k][:, W * c : W * (c + 1)], in_=acc[k % 2][c][:, W:N], func=ACT.Relu, bias=bias(k, c))
 
-        def square_v(g):
-            nc.vector.tensor_tensor(out=res[g][:], in0=relu[g][:], in1=relu[g][:], op=ALU.mult)
-            nc.sync.dma_start(out=out[g], in_=res[g][:])
+        def square_v(k, c0, c1):
+            t = relu[k][:, W * c0 : W * c1]
+            nc.vector.tensor_tensor(out=res[k][:, W * c0 : W * c1], in0=t, in1=t, op=ALU.mult)
 
-        def square_s(g):
-            nc.scalar.activation(out=res[g][:], in_=relu[g][:], func=ACT.Square)
-            nc.sync.dma_start(out=out[g], in_=res[g][:])
+        def square_s(k, c0, c1):
+            nc.scalar.activation(out=res[k][:, W * c0 : W * c1], in_=relu[k][:, W * c0 : W * c1], func=ACT.Square)
 
-        interleave(nc.scalar.copy, 0, 320, 512)
-        interleave(nc.vector.tensor_copy, 0, 0, 256)
-        interleave(nc.vector.tensor_copy, 0, 256, 320)
-        quantize(0, 0, 256)
-        quantize(0, 256, 512)
-        multiply(0)
+        def store(k, c0, c1):
+            g0 = TILES * (k // 2)
+            nc.sync.dma_start(
+                out=out[g0 + c0 : g0 + c1, :, W * (k % 2) : W * (k % 2 + 1)].rearrange("g m n -> m g n"),
+                in_=res[k][:, W * c0 : W * c1].rearrange("m (g n) -> m g n", n=W),
+            )
 
-        relu_v(0)
-        relu_s(1)
-        square_s(0)
-        interleave(nc.vector.tensor_copy, 1, 0, 256)
-        interleave(nc.vector.tensor_copy, 1, 256, 512)
-        quantize(1, 0, 256)
-        quantize(1, 256, 512)
-        multiply(1)
-        relu_s(2)
-        square_s(1)
-        relu_v(3)
-        square_s(2)
-        relu_v(4)
-        square_s(3)
-        relu_v(5)
-        square_s(4)
-        relu_v(6)
-        square_s(5)
-        relu_v(7)
-        square_s(6)
-        square_v(7)
+
+        interleave(nc.scalar.copy, 0, W - 96, W)
+        interleave(nc.vector.tensor_copy, 0, 0, W - 96)
+        quantize_and_multiply(0)
+        nc.vector.transpose(b_cols[:], b_rows[:])
+        interleave(nc.scalar.copy, 1, W - 96, W)
+        for k in range(CHUNKS):
+            if k == 0:
+                interleave(nc.vector.tensor_copy, 1, 0, W - 96)
+            elif k + 1 < CHUNKS:
+                interleave(nc.vector.tensor_copy, k + 1, 0, W)
+            relu_v(k, 0)
+            if k + 1 < CHUNKS:
+                quantize_and_multiply(k + 1)
+            relu_s(k, 1)
+            relu_s(k, 2)
+            relu_v(k, 3)
+            if k < 2:
+                square_s(k, 0, 2)
+            else:
+                square_v(k, 0, 2)
+            store(k, 0, 2)
+            if k + 1 < CHUNKS:
+                square_s(k, 2, 4)
+                store(k, 2, 4)
+            else:
+                square_s(k, 2, 3)
+                store(k, 2, 3)
+                square_v(k, 3, 4)
+                store(k, 3, 4)

@@ -35,7 +35,7 @@ def tile_rows_glin_relu2_bias_kernel(tc, x, w_words, w_scales, b, out):
         grouped = [keep.tile([P, PACK * W], BF16, name="grouped%d" % k, align_bytes=64) for k in range(CHUNKS)]
         codes = keep.tile([P, (CHUNKS + 1) * W], U32, align_bytes=64)
         scales = keep.tile([P, (CHUNKS + 1) * W], U8, align_bytes=64)
-        w_sb = keep.tile([P, SETS, 2 * M], U8, align_bytes=64)
+        w_sb = [keep.tile([P, 2 * M], U8, name="w%d" % s, align_bytes=64) for s in range(SETS)]
         ws_sb = keep.tile([P, SETS, M], U8, align_bytes=64)
         b_rows = keep.tile([P, G * ROWS], F32, align_bytes=64)
         b_cols = keep.tile([P, G * ROWS], F32, align_bytes=64)
@@ -44,26 +44,32 @@ def tile_rows_glin_relu2_bias_kernel(tc, x, w_words, w_scales, b, out):
         res = [keep.tile([M, TILES * W], F32, name="res%d" % k) for k in range(CHUNKS)]
 
         x_sets = x.rearrange("(s c) (p j) n -> s (c p) j n", c=TILES, j=PACK)
+        w_sets = w_words.rearrange("(s c) p v -> s (c p) v", c=TILES)
         ws_tiles = w_scales.rearrange("(s c) f m -> c f s m", c=TILES)
 
         nc.vector.memset(ws_sb[:].bitcast(U32), 0)
-        nc.vector.memset(b_rows[:], 0.0)
+        nc.gpsimd.memset(b_rows[:], 0.0)
         nc.vector.memset(codes[:, 0:W], 0)
         nc.vector.memset(scales[:, 0:W].bitcast(U32), 0)
 
         def load_x(k):
             nc.sync.dma_start(out=raw[k][:], in_=x_sets[k // 2][:, :, W * (k % 2) : W * (k % 2 + 1)])
 
+        def load_w(s):
+            nc.sync.dma_start(out=w_sb[s][:].bitcast(I32), in_=w_sets[s].bitcast(I32))
+
         load_x(0)
-        nc.sync.dma_start(out=w_sb[:].bitcast(I32), in_=w_words.rearrange("(s c) p v -> (c p) s v", c=TILES).bitcast(I32))
+        load_w(0)
         for c in range(TILES):
             nc.sync.dma_start(out=ws_sb[ROWS * c : ROWS * c + 4].bitcast(I32), in_=ws_tiles[c].bitcast(I32))
-        nc.scalar.dma_start(
+        nc.gpsimd.dma_start(
             out=b_rows[0:P:ROWS, :].rearrange("q (g a) -> q g a", a=ROWS),
             in_=b.rearrange("g (q a) o -> q g (a o)", a=ROWS),
         )
-        for k in range(1, CHUNKS):
-            load_x(k)
+        load_x(1)
+        load_x(2)
+        load_w(1)
+        load_x(3)
 
         def interleave(copy, k, n0, n1):
             dst = grouped[k][:].rearrange("p (c i t) -> p c t i", i=4, t=PACK)
@@ -81,7 +87,7 @@ def tile_rows_glin_relu2_bias_kernel(tc, x, w_words, w_scales, b, out):
                 rows = slice(ROWS * c, ROWS * (c + 1))
                 nc.tensor.matmul_mx(
                     out=acc[k % 2][c][:],
-                    lhsT=w_sb[rows, k // 2, :].bitcast(FP4X4),
+                    lhsT=w_sb[k // 2][rows, :].bitcast(FP4X4),
                     lhsT_scale=ws_sb[rows, k // 2, :],
                     rhs=codes[rows, window].bitcast(FP8X4),
                     rhs_scale=scales[rows, window],
@@ -128,18 +134,20 @@ def tile_rows_glin_relu2_bias_kernel(tc, x, w_words, w_scales, b, out):
             if k + 1 < CHUNKS:
                 quantize_and_multiply(k + 1)
             relu_s(k, 1)
-            relu_s(k, 2)
-            relu_v(k, 3)
             if k < 2:
-                square_s(k, 0, 2)
-            else:
-                square_v(k, 0, 2)
-            store(k, 0, 2)
-            if k + 1 < CHUNKS:
-                square_s(k, 2, 4)
-                store(k, 2, 4)
-            else:
+                relu_s(k, 2)
+                square_s(k, 0, 1)
+                square_v(k, 1, 2)
+                store(k, 0, 2)
+                relu_s(k, 3)
                 square_s(k, 2, 3)
-                store(k, 2, 3)
+                square_s(k, 3, 4)
+            else:
+                relu_v(k, 2)
+                relu_s(k, 3)
+                square_s(k, 0, 1)
+                square_v(k, 1, 2)
+                store(k, 0, 2)
+                square_s(k, 2, 3)
                 square_v(k, 3, 4)
-                store(k, 3, 4)
+            store(k, 2, 4)

@@ -48,7 +48,7 @@ def tile_rows_glin_relu2_bias_kernel(tc, x, w_words, w_scales, b, out):
         ws_tiles = w_scales.rearrange("(s c) f m -> c f s m", c=TILES)
 
         nc.vector.memset(ws_sb[:].bitcast(U32), 0)
-        nc.gpsimd.memset(b_rows[:], 0.0)
+        nc.vector.memset(b_rows[:], 0.0)
         nc.vector.memset(codes[:, 0:W], 0)
         nc.vector.memset(scales[:, 0:W].bitcast(U32), 0)
 
@@ -62,7 +62,7 @@ def tile_rows_glin_relu2_bias_kernel(tc, x, w_words, w_scales, b, out):
         load_w(0)
         for c in range(TILES):
             nc.sync.dma_start(out=ws_sb[ROWS * c : ROWS * c + 4].bitcast(I32), in_=ws_tiles[c].bitcast(I32))
-        nc.gpsimd.dma_start(
+        nc.scalar.dma_start(
             out=b_rows[0:P:ROWS, :].rearrange("q (g a) -> q g a", a=ROWS),
             in_=b.rearrange("g (q a) o -> q g (a o)", a=ROWS),
         )

@@ -82,11 +82,14 @@ def tile_rows_glin_relu2_bias_kernel(tc, x, w_words, w_scales, b, out):
                 scales=scales[:, W * (k + 1) : W * (k + 2)],
                 in_=grouped[k][:],
             )
+            multiply(k, k % 2)
+
+        def multiply(k, bank):
             window = slice(W * k, W * k + N)
             for c in range(TILES):
                 rows = slice(ROWS * c, ROWS * (c + 1))
                 nc.tensor.matmul_mx(
-                    out=acc[k % 2][c][:],
+                    out=acc[bank][c][:],
                     lhsT=w_sb[k // 2][rows, :].bitcast(FP4X4),
                     lhsT_scale=ws_sb[rows, k // 2, :],
                     rhs=codes[rows, window].bitcast(FP8X4),
@@ -123,6 +126,7 @@ def tile_rows_glin_relu2_bias_kernel(tc, x, w_words, w_scales, b, out):
         interleave(nc.scalar.copy, 0, W - 96, W)
         interleave(nc.vector.tensor_copy, 0, 0, W - 96)
         quantize_and_multiply(0)
+        multiply(0, 1)
         nc.vector.transpose(b_cols[:], b_rows[:])
         interleave(nc.scalar.copy, 1, W - 96, W)
         for k in range(CHUNKS):
@@ -151,3 +155,6 @@ def tile_rows_glin_relu2_bias_kernel(tc, x, w_words, w_scales, b, out):
                 square_s(k, 2, 3)
                 square_v(k, 3, 4)
             store(k, 2, 4)
+            if k + 2 < CHUNKS:
+                for rep in range(k + 1):
+                    multiply(k + 1, k % 2)

from contextlib import ExitStack

import concourse.mybir as mybir

G, D, M, N = 8, 128, 128, 512
FLOPS = 2 * G * D * M * N

F32 = mybir.dt.float32
BF16 = mybir.dt.bfloat16
I32 = mybir.dt.int32
U32 = mybir.dt.uint32
U8 = mybir.dt.uint8
FP8X4 = mybir.dt.float8_e4m3fn_x4
FP4X4 = mybir.dt.float4_e2m1fn_x4
ALU = mybir.AluOpType
ACT = mybir.ActivationFunctionType

P = 128
PACK = 4
ROWS = 32
TILES = 4
SETS = 2
W = 256
CHUNKS = 4


def tile_rows_glin_relu2_bias_kernel(tc, x, w_words, w_scales, b, out):
    nc = tc.nc
    with ExitStack() as ctx:
        keep = ctx.enter_context(tc.tile_pool(name="keep", bufs=1))
        psum = ctx.enter_context(tc.psum_pool(name="psum", bufs=1))
        ctx.enter_context(tc.manual_schedule())

        raw = [keep.tile([P, PACK, W], F32, name="raw%d" % k) for k in range(CHUNKS)]
        grouped = [keep.tile([P, PACK * W], BF16, name="grouped%d" % k, align_bytes=64) for k in range(CHUNKS)]
        codes = keep.tile([P, (CHUNKS + 1) * W], U32, align_bytes=64)
        scales = keep.tile([P, (CHUNKS + 1) * W], U8, align_bytes=64)
        w_sb = [keep.tile([P, 2 * M], U8, name="w%d" % s, align_bytes=64) for s in range(SETS)]
        ws_sb = keep.tile([P, SETS, M], U8, align_bytes=64)
        b_rows = keep.tile([P, G * ROWS], F32, align_bytes=64)
        b_cols = keep.tile([P, G * ROWS], F32, align_bytes=64)
        acc = [[psum.tile([M, N], F32, name="acc%d_%d" % (h, c)) for c in range(TILES)] for h in range(2)]
        relu = [keep.tile([M, TILES * W], F32, name="relu%d" % k) for k in range(CHUNKS)]
        res = [keep.tile([M, TILES * W], F32, name="res%d" % k) for k in range(CHUNKS)]

        x_sets = x.rearrange("(s c) (p j) n -> s (c p) j n", c=TILES, j=PACK)
        w_sets = w_words.rearrange("(s c) p v -> s (c p) v", c=TILES)
        ws_tiles = w_scales.rearrange("(s c) f m -> c f s m", c=TILES)

        nc.vector.memset(ws_sb[:].bitcast(U32), 0)
        nc.vector.memset(b_rows[:], 0.0)
        nc.vector.memset(codes[:, 0:W], 0)
        nc.vector.memset(scales[:, 0:W].bitcast(U32), 0)

        def load_x(k):
            nc.sync.dma_start(out=raw[k][:], in_=x_sets[k // 2][:, :, W * (k % 2) : W * (k % 2 + 1)])

        def load_w(s):
            nc.sync.dma_start(out=w_sb[s][:].bitcast(I32), in_=w_sets[s].bitcast(I32))

        load_x(0)
        load_w(0)
        for c in range(TILES):
            nc.sync.dma_start(out=ws_sb[ROWS * c : ROWS * c + 4].bitcast(I32), in_=ws_tiles[c].bitcast(I32))
        nc.scalar.dma_start(
            out=b_rows[0:P:ROWS, :].rearrange("q (g a) -> q g a", a=ROWS),
            in_=b.rearrange("g (q a) o -> q g (a o)", a=ROWS),
        )
        load_x(1)
        load_x(2)
        load_w(1)
        load_x(3)

        def interleave(copy, k, n0, n1):
            dst = grouped[k][:].rearrange("p (c i t) -> p c t i", i=4, t=PACK)
            src = raw[k][:].rearrange("p t (c i) -> p c t i", i=4)
            copy(out=dst[:, n0 // 4 : n1 // 4], in_=src[:, n0 // 4 : n1 // 4])

        def quantize_and_multiply(k):
            nc.vector.quantize_mx(
                out=codes[:, W * (k + 1) : W * (k + 2)].bitcast(FP8X4),
                scales=scales[:, W * (k + 1) : W * (k + 2)],
                in_=grouped[k][:],
            )
            multiply(k, k % 2)

        def multiply(k, bank):
            window = slice(W * k, W * k + N)
            for c in range(TILES):
                rows = slice(ROWS * c, ROWS * (c + 1))
                nc.tensor.matmul_mx(
                    out=acc[bank][c][:],
                    lhsT=w_sb[k // 2][rows, :].bitcast(FP4X4),
                    lhsT_scale=ws_sb[rows, k // 2, :],
                    rhs=codes[rows, window].bitcast(FP8X4),
                    rhs_scale=scales[rows, window],
                    start=True,
                    stop=True,
                )

        def bias(k, c):
            g = TILES * (k // 2) + c
            return b_cols[:, ROWS * g : ROWS * g + 1]

        def relu_v(k, c):
            nc.vector.tensor_scalar(out=relu[k][:, W * c : W * (c + 1)], in0=acc[k % 2][c][:, W:N], scalar1=bias(k, c), scalar2=0.0, op0=ALU.add, op1=ALU.max)

        def relu_s(k, c):
            nc.scalar.activation(out=relu[k][:, W * c : W * (c + 1)], in_=acc[k % 2][c][:, W:N], func=ACT.Relu, bias=bias(k, c))

        def square_v(k, c0, c1):
            t = relu[k][:, W * c0 : W * c1]
            nc.vector.tensor_tensor(out=res[k][:, W * c0 : W * c1], in0=t, in1=t, op=ALU.mult)

        def square_s(k, c0, c1):
            nc.scalar.activation(out=res[k][:, W * c0 : W * c1], in_=relu[k][:, W * c0 : W * c1], func=ACT.Square)

        def store(k, c0, c1):
            g0 = TILES * (k // 2)
            nc.sync.dma_start(
                out=out[g0 + c0 : g0 + c1, :, W * (k % 2) : W * (k % 2 + 1)].rearrange("g m n -> m g n"),
                in_=res[k][:, W * c0 : W * c1].rearrange("m (g n) -> m g n", n=W),
            )


        interleave(nc.scalar.copy, 0, W - 96, W)
        interleave(nc.vector.tensor_copy, 0, 0, W - 96)
        quantize_and_multiply(0)
        multiply(0, 1)
        nc.vector.transpose(b_cols[:], b_rows[:])
        interleave(nc.scalar.copy, 1, W - 96, W)
        for k in range(CHUNKS):
            if k == 0:
                interleave(nc.vector.tensor_copy, 1, 0, W - 96)
            elif k + 1 < CHUNKS:
                interleave(nc.vector.tensor_copy, k + 1, 0, W)
            relu_v(k, 0)
            if k + 1 < CHUNKS:
                quantize_and_multiply(k + 1)
            relu_s(k, 1)
            if k < 2:
                relu_s(k, 2)
                square_s(k, 0, 1)
                square_v(k, 1, 2)
                store(k, 0, 2)
                relu_s(k, 3)
                square_s(k, 2, 3)
                square_s(k, 3, 4)
            else:
                relu_v(k, 2)
                relu_s(k, 3)
                square_s(k, 0, 1)
                square_v(k, 1, 2)
                store(k, 0, 2)
                square_s(k, 2, 3)
                square_v(k, 3, 4)
            store(k, 2, 4)
            if k + 2 < CHUNKS:
                for rep in range(k + 1):
                    multiply(k + 1, k % 2)
